import numpy as np, ml_dtypes
CORES = [25,29,65,69,153,157,193,197]
N = 8
import mx_ref
NC = 128
BF = ml_dtypes.bfloat16
def setup_inputs(rng):
    def f(*shape):
        return mx_ref.flush((rng.standard_normal(shape, dtype=np.float32) * np.exp2(rng.integers(-2, 3, shape[:-1] + (1,)))).astype(BF))
    return {"w": f(N, 128, 512), "x": f(N, 128, N * 4 * NC)}
def setup_inputs_blocks(rng):
    d = setup_inputs(rng)
    for k in ("w", "x"): d[k] = mx_ref.spread(d[k], rng, 4)
    return d
def setup_inputs_wide(rng):
    d = setup_inputs(rng)
    for k in ("w", "x"): d[k] = mx_ref.flush((d[k].astype(np.float32) * np.exp2(rng.integers(-8, 9, (N, 1, 1))).astype(np.float32)).astype(BF))
    return d
def setup_inputs_zeros(rng):
    d = setup_inputs(rng); v = d["x"].reshape(N, 128, -1, 4).copy()
    v[np.broadcast_to((rng.random((N, 1, v.shape[2], 1)) < 0.33), v.shape)] = 0
    d["x"] = v.reshape(d["x"].shape)
    return d
def reference(w, x):
    y = np.zeros((N, 128, N * NC), np.float32)
    for r in range(N):
        qw = mx_ref.quantize(w[r])
        for j in range(N):
            y[r][:, NC * j:NC * j + NC] = mx_ref.matmul(qw, mx_ref.quantize(x[j][:, 4 * NC * r:4 * NC * r + 4 * NC]))
    return {"y": y}

@@ -1,0 +1,185 @@
+from concourse.bass import DstId, RemoteDMATransfer
+from concourse.mybir import dt, ActivationFunctionType
+
+N = 8
+NG = 4
+WORLD = 256
+XC = 512
+QC = 128
+BANK = 512
+
+SCRATCH = {
+    "xb": ("sbuf", [128, N * XC], "bfloat16"),
+    "wb": ("sbuf", [128, XC], "bfloat16"),
+    "xq": ("sbuf", [128, N * QC], "float8_e4m3fn_x4"),
+    "xs": ("sbuf", [128, N * QC], "uint8"),
+    "wq": ("sbuf", [128, QC], "float8_e4m3fn_x4"),
+    "ws": ("sbuf", [128, QC], "uint8"),
+    "rq": ("sbuf", [128, N * QC], "float8_e4m3fn_x4"),
+    "rs": ("sbuf", [128, N * QC], "uint8"),
+    "ps": ("psum", [128, NG * BANK], "float32"),
+    "yb": ("sbuf", [128, N * QC], "float32"),
+}
+SEMAPHORES = (["ld%d" % k for k in range(NG)] + ["qd%d" % k for k in range(NG)] + ["arr%d" % k for k in range(NG)]
+              + ["mm%d" % k for k in range(NG)] + ["cp%d" % k for k in range(NG)]
+              + ["ldw", "qw", "qme", "hs", "hq", "sent", "st"])
+
+
+def _count(mask):
+    return bin(mask).count("1")
+
+
+def _plan(cores, topo):
+    groups = []
+    for r, c in enumerate(cores):
+        for gr in groups:
+            if topo.host(cores[gr[0]]) == topo.host(c) and topo.chip(cores[gr[0]]) == topo.chip(c):
+                gr.append(r)
+                break
+        else:
+            groups.append([r])
+    relay, taken = {}, set(cores)
+    for j, c in enumerate(cores):
+        for k, gr in enumerate(groups):
+            if all(topo.may_write(c, cores[d]) for d in gr):
+                continue
+            idle = [h for h in range(WORLD) if h not in taken
+                    and topo.host(h) == topo.host(c) and topo.chip(h) == topo.chip(c)
+                    and all(topo.may_write(h, cores[d]) for d in gr)]
+            idle.sort(key=lambda h: topo.die(h) != topo.die(c))
+            relay[(j, k)] = idle[0]
+            taken.add(idle[0])
+    return groups, relay
+
+
+def _split(topo, src, dsts):
+    masks, taken = {}, 0
+    for m in sorted(set(topo.mask(src, d) for d in dsts), key=_count):
+        those = [d for d in dsts if topo.mask(src, d) == m]
+        free = [b for b in range(m.bit_length()) if ((m & ~taken) >> b) & 1]
+        n = 1
+        while 2 * n * len(those) <= len(free):
+            n *= 2
+        for i, d in enumerate(those):
+            masks[d] = sum(1 << b for b in free[i * n:(i + 1) * n])
+            taken |= masks[d]
+    return masks
+
+
+def _own_dsts(cores, groups, relay, j):
+    return [d for k, gr in enumerate(groups) if (j, k) not in relay for d in gr if d != j]
+
+
+def _last_hop(cores, topo, groups, relay, j, k):
+    if (j, k) in relay:
+        return _split(topo, relay[(j, k)], [cores[d] for d in groups[k]])
+    return _split(topo, cores[j], [cores[d] for d in _own_dsts(cores, groups, relay, j)])
+
+
+def _codes(buf, lo, hi):
+    return buf[:, QC * lo:QC * hi].bitcast(dt.uint8)
+
+
+def _plane(buf, lo, hi):
+    return buf[:, QC * lo:QC * hi]
+
+
+def _xfer(topo, src_core, dst_core, mask, sem, src, dst):
+    rid, pid = topo.addr(dst_core, src_core)
+    return RemoteDMATransfer(dst_ids=[DstId(rid=rid, pnc=pid)], dma_engine_mask=mask, remote_sem=sem, src=src, dst=dst)
+
+
+def _helper(g, core, T, topo, cores, groups, j, k, landed):
+    masks = _split(topo, core, [cores[d] for d in groups[k]])
+    kj = [i for i, gr in enumerate(groups) if j in gr][0]
+    arr = T.sem["arr%d" % kj]
+    left = 0
+    for view, here, there, sem in ((_plane, T.xs, T.rs, T.sem.hs), (_codes, T.xq, T.rq, T.sem.hq)):
+        g.wait_ge(sem, landed)
+        g.remote_dma_fused([_xfer(topo, core, cores[d], masks[cores[d]], arr, view(here, d, d + 1), view(there, j, j + 1))
+                            for d in groups[k]], local_sem=T.sem.sent)
+        left += sum(_count(masks[cores[d]]) for d in groups[k])
+    g.wait_ge(T.sem.sent, left)
+
+
+def rank_program(g, core, T, topo):
+    cores = [int(c) for c in T.cores]
+    groups, relay = _plan(cores, topo)
+
+    for (j, k), h in relay.items():
+        if h == core:
+            to_helpers = _split(topo, cores[j], [relay[(j, kk)] for kk in range(len(groups)) if (j, kk) in relay])
+            _helper(g, core, T, topo, cores, groups, j, k, _count(to_helpers[core]))
+            return
+    r = T.rank_of(core)
+    if r is None:
+        return
+
+    span = [(gr[0], gr[-1] + 1) for gr in groups]
+    own = [k for k, gr in enumerate(groups) if r in gr][0]
+    far = [k for k in range(len(groups)) if (r, k) in relay]
+    near = [k for k in range(len(groups)) if k != own and k not in far]
+    peers = [d for d in groups[own] if d != r]
+    hw = (g.sync, g.scalar)
+
+    for i, k in enumerate(far + near + [own]):
+        lo, hi = span[k]
+        hw[i % 2].dma_start(T.xb[:, XC * lo:XC * hi], T.x[:, XC * lo:XC * hi]).then_inc(T.sem["ld%d" % k], 16)
+    hw[len(groups) % 2].dma_start(T.wb[:], T.w[:]).then_inc(T.sem.ldw, 16)
+
+    for k in far + near:
+        lo, hi = span[k]
+        g.vector.wait_ge(T.sem["ld%d" % k], 16)
+        g.vector.quantize_mx(T.xq[:, QC * lo:QC * hi], T.xs[:, QC * lo:QC * hi],
+                             T.xb[:, XC * lo:XC * hi]).then_inc(T.sem["qd%d" % k], 1)
+    g.vector.wait_ge(T.sem["ld%d" % own], 16)
+    for d in peers:
+        g.vector.quantize_mx(T.xq[:, QC * d:QC * (d + 1)], T.xs[:, QC * d:QC * (d + 1)],
+                             T.xb[:, XC * d:XC * (d + 1)]).then_inc(T.sem["qd%d" % own], 1)
+    g.vector.quantize_mx(T.rq[:, QC * r:QC * (r + 1)], T.rs[:, QC * r:QC * (r + 1)],
+                         T.xb[:, XC * r:XC * (r + 1)]).then_inc(T.sem.qme, 1)
+    g.vector.wait_ge(T.sem.ldw, 16)
+    g.vector.quantize_mx(T.wq[:], T.ws[:], T.wb[:]).then_inc(T.sem.qw, 1)
+
+    left = 0
+    for k in far:
+        g.wait_ge(T.sem["qd%d" % k], 1)
+    masks = _split(topo, core, [relay[(r, k)] for k in far])
+    for view, buf, sem in ((_plane, T.xs, T.sem.hs), (_codes, T.xq, T.sem.hq)):
+        g.remote_dma_fused([_xfer(topo, core, relay[(r, k)], masks[relay[(r, k)]], sem,
+                                  view(buf, span[k][0], span[k][1]), view(buf, span[k][0], span[k][1]))
+                            for k in far], local_sem=T.sem.sent)
+        left += sum(_count(masks[relay[(r, k)]]) for k in far)
+    for k in near:
+        g.wait_ge(T.sem["qd%d" % k], 1)
+    g.wait_ge(T.sem["qd%d" % own], len(peers))
+    dsts = _own_dsts(cores, groups, relay, r)
+    masks = _split(topo, core, [cores[d] for d in dsts])
+    for view, here, there in ((_codes, T.xq, T.rq), (_plane, T.xs, T.rs)):
+        g.remote_dma_fused([_xfer(topo, core, cores[d], masks[cores[d]], T.sem["arr%d" % own],
+                                  view(here, d, d + 1), view(there, r, r + 1))
+                            for d in dsts], local_sem=T.sem.sent)
+        left += sum(_count(masks[cores[d]]) for d in dsts)
+
+    g.tensor.wait_ge(T.sem.qw, 1)
+    for i, k in enumerate([own] + near + far):
+        lo, hi = span[k]
+        due = sum(2 * _count(_last_hop(cores, topo, groups, relay, j, own)[core]) for j in groups[k] if j != r)
+        g.tensor.wait_ge(T.sem["arr%d" % k], due)
+        if k == own:
+            g.tensor.wait_ge(T.sem.qme, 1)
+        bank = T.ps[:, BANK * k:BANK * k + QC * (hi - lo)]
+        g.tensor.matmul_mx(bank, T.wq[:], T.ws[:], T.rq[:, QC * lo:QC * hi], T.rs[:, QC * lo:QC * hi],
+                           True, True).then_inc(T.sem["mm%d" % k], 1)
+        out = T.yb[:, QC * lo:QC * hi]
+        if i % 2 == 0:
+            g.vector.wait_ge(T.sem["mm%d" % k], 1)
+            g.vector.tensor_copy(out, bank).then_inc(T.sem["cp%d" % k], 1)
+        else:
+            g.scalar.wait_ge(T.sem["mm%d" % k], 1)
+            g.scalar.activation(out, bank, ActivationFunctionType.Copy).then_inc(T.sem["cp%d" % k], 1)
+        hw[i % 2].wait_ge(T.sem["cp%d" % k], 1)
+        hw[i % 2].dma_start(T.y[:, QC * lo:QC * hi], out).then_inc(T.sem.st, 16)
+
+    g.wait_ge(T.sem.sent, left)
+    g.wait_ge(T.sem.st, 16 * len(groups))

@@ -3,6 +3,7 @@ from concourse.mybir import dt, ActivationFunctionType
 
 N = 8
 NG = 4
+NP = 6
 WORLD = 256
 XC = 512
 QC = 128
@@ -17,12 +18,12 @@ SCRATCH = {
     "ws": ("sbuf", [128, QC], "uint8"),
     "rq": ("sbuf", [128, N * QC], "float8_e4m3fn_x4"),
     "rs": ("sbuf", [128, N * QC], "uint8"),
-    "ps": ("psum", [128, NG * BANK], "float32"),
+    "ps": ("psum", [128, N * BANK], "float32"),
     "yb": ("sbuf", [128, N * QC], "float32"),
 }
-SEMAPHORES = (["ld%d" % k for k in range(NG)] + ["qd%d" % k for k in range(NG)] + ["arr%d" % k for k in range(NG)]
-              + ["mm%d" % k for k in range(NG)] + ["cp%d" % k for k in range(NG)]
-              + ["ldw", "qw", "qme", "hs", "hq", "sent", "st"])
+SEMAPHORES = (["ld%d" % i for i in range(NP)] + ["qd%d" % i for i in range(NP)] + ["arr%d" % k for k in range(NG)]
+              + ["mm%d" % j for j in range(N)] + ["cp%d" % j for j in range(N)]
+              + ["ldw", "qw", "qme", "hlead", "hrest", "hcodes", "sent", "st"])
 
 
 def _count(mask):
@@ -66,120 +67,130 @@ def _split(topo, src, dsts):
     return masks
 
 
-def _own_dsts(cores, groups, relay, j):
-    return [d for k, gr in enumerate(groups) if (j, k) not in relay for d in gr if d != j]
+def _roles(cores, topo, groups, relay, j):
+    own = [k for k, gr in enumerate(groups) if j in gr][0]
+    far = [k for k in range(len(groups)) if (j, k) in relay]
+    far.sort(key=lambda k: topo.host(cores[groups[k][0]]) != topo.host(cores[j]))
+    near = [k for k in range(len(groups)) if k != own and k not in far]
+    pieces = ([(groups[k][0], groups[k][0] + 1) for k in far] + [(groups[k][1], groups[k][-1] + 1) for k in far]
+              + [(groups[k][0], groups[k][-1] + 1) for k in near + [own]])
+    return own, far, near, pieces
 
 
-def _last_hop(cores, topo, groups, relay, j, k):
-    if (j, k) in relay:
-        return _split(topo, relay[(j, k)], [cores[d] for d in groups[k]])
-    return _split(topo, cores[j], [cores[d] for d in _own_dsts(cores, groups, relay, j)])
+def _remote_calls(cores, topo, groups, relay):
+    calls = {}
+    for j, c in enumerate(cores):
+        own, far, near, pieces = _roles(cores, topo, groups, relay, j)
+        nf = len(far)
+        mine = []
+        for i, k in enumerate(far):
+            lo, hi = pieces[i]
+            h = relay[(j, k)]
+            mine.append(([("qd%d" % i, 1)], [(h, topo.mask(c, h), "hlead", "s", lo, hi, "x", lo)]))
+        m = _split(topo, c, [relay[(j, k)] for k in far])
+        mine.append(([("qd%d" % (nf + i), 1) for i in range(nf)],
+                     [(relay[(j, k)], m[relay[(j, k)]], "hrest", "s", pieces[nf + i][0], pieces[nf + i][1], "x", pieces[nf + i][0])
+                      for i, k in enumerate(far)]))
+        mine.append(([], [(relay[(j, k)], m[relay[(j, k)]], "hcodes", "q", groups[k][0], groups[k][-1] + 1, "x", groups[k][0])
+                          for k in far]))
+        dsts = [d for k in near + [own] for d in groups[k] if d != j]
+        m = _split(topo, c, [cores[d] for d in dsts])
+        waits = [("qd%d" % (2 * nf + i), 1) for i in range(len(near))] + [("qd%d" % (2 * nf + len(near)), len(groups[own]) - 1)]
+        for kind in "qs":
+            mine.append((waits, [(cores[d], m[cores[d]], "arr%d" % own, kind, d, d + 1, "r", j) for d in dsts]))
+            waits = []
+        calls[c] = mine
+        for k in far:
+            h, gr = relay[(j, k)], groups[k]
+            arr = "arr%d" % own
+            rest = _split(topo, h, [cores[d] for d in gr[1:]])
+            both = _split(topo, h, [cores[d] for d in gr])
+            calls[h] = [([("hlead", None)], [(cores[gr[0]], topo.mask(h, cores[gr[0]]), arr, "s", gr[0], gr[0] + 1, "r", j)]),
+                        ([("hrest", None)], [(cores[d], rest[cores[d]], arr, "s", d, d + 1, "r", j) for d in gr[1:]]),
+                        ([("hcodes", None)], [(cores[d], both[cores[d]], arr, "q", d, d + 1, "r", j) for d in gr])]
+    landed = {}
+    for c in calls:
+        for waits, transfers in calls[c]:
+            for t in transfers:
+                landed[(t[0], t[2])] = landed.get((t[0], t[2]), 0) + _count(t[1])
+    return calls, landed
 
 
-def _codes(buf, lo, hi):
-    return buf[:, QC * lo:QC * hi].bitcast(dt.uint8)
+def _view(buf, kind, lo, hi):
+    return buf[:, QC * lo:QC * hi].bitcast(dt.uint8) if kind == "q" else buf[:, QC * lo:QC * hi]
 
 
-def _plane(buf, lo, hi):
-    return buf[:, QC * lo:QC * hi]
-
-
-def _xfer(topo, src_core, dst_core, mask, sem, src, dst):
-    rid, pid = topo.addr(dst_core, src_core)
-    return RemoteDMATransfer(dst_ids=[DstId(rid=rid, pnc=pid)], dma_engine_mask=mask, remote_sem=sem, src=src, dst=dst)
-
-
-def _helper(g, core, T, topo, cores, groups, j, k, landed):
-    masks = _split(topo, core, [cores[d] for d in groups[k]])
-    kj = [i for i, gr in enumerate(groups) if j in gr][0]
-    arr = T.sem["arr%d" % kj]
+def _issue(g, core, T, topo, calls, landed):
     left = 0
-    for view, here, there, sem in ((_plane, T.xs, T.rs, T.sem.hs), (_codes, T.xq, T.rq, T.sem.hq)):
-        g.wait_ge(sem, landed)
-        g.remote_dma_fused([_xfer(topo, core, cores[d], masks[cores[d]], arr, view(here, d, d + 1), view(there, j, j + 1))
-                            for d in groups[k]], local_sem=T.sem.sent)
-        left += sum(_count(masks[cores[d]]) for d in groups[k])
-    g.wait_ge(T.sem.sent, left)
+    for waits, transfers in calls[core]:
+        for name, count in waits:
+            g.wait_ge(T.sem[name], landed[(core, name)] if count is None else count)
+        made = []
+        for dst, mask, sem, kind, lo, hi, there, at in transfers:
+            rid, pid = topo.addr(dst, core)
+            made.append(RemoteDMATransfer(dst_ids=[DstId(rid=rid, pnc=pid)], dma_engine_mask=mask, remote_sem=T.sem[sem],
+                                          src=_view(T["x" + kind], kind, lo, hi),
+                                          dst=_view(T[there + kind], kind, at, at + hi - lo)))
+            left += _count(mask)
+        g.remote_dma_fused(made, local_sem=T.sem.sent)
+    return left
 
 
 def rank_program(g, core, T, topo):
     cores = [int(c) for c in T.cores]
     groups, relay = _plan(cores, topo)
-
-    for (j, k), h in relay.items():
-        if h == core:
-            to_helpers = _split(topo, cores[j], [relay[(j, kk)] for kk in range(len(groups)) if (j, kk) in relay])
-            _helper(g, core, T, topo, cores, groups, j, k, _count(to_helpers[core]))
-            return
+    calls, landed = _remote_calls(cores, topo, groups, relay)
+    if core not in calls:
+        return
     r = T.rank_of(core)
     if r is None:
+        g.wait_ge(T.sem.sent, _issue(g, core, T, topo, calls, landed))
         return
 
-    span = [(gr[0], gr[-1] + 1) for gr in groups]
-    own = [k for k, gr in enumerate(groups) if r in gr][0]
-    far = [k for k in range(len(groups)) if (r, k) in relay]
-    near = [k for k in range(len(groups)) if k != own and k not in far]
-    peers = [d for d in groups[own] if d != r]
+    own, far, near, pieces = _roles(cores, topo, groups, relay, r)
     hw = (g.sync, g.scalar)
 
-    for i, k in enumerate(far + near + [own]):
-        lo, hi = span[k]
-        hw[i % 2].dma_start(T.xb[:, XC * lo:XC * hi], T.x[:, XC * lo:XC * hi]).then_inc(T.sem["ld%d" % k], 16)
-    hw[len(groups) % 2].dma_start(T.wb[:], T.w[:]).then_inc(T.sem.ldw, 16)
+    for i, (lo, hi) in enumerate(pieces):
+        hw[i % 2].dma_start(T.xb[:, XC * lo:XC * hi], T.x[:, XC * lo:XC * hi]).then_inc(T.sem["ld%d" % i], 16)
+    hw[len(pieces) % 2].dma_start(T.wb[:], T.w[:]).then_inc(T.sem.ldw, 16)
 
-    for k in far + near:
-        lo, hi = span[k]
-        g.vector.wait_ge(T.sem["ld%d" % k], 16)
-        g.vector.quantize_mx(T.xq[:, QC * lo:QC * hi], T.xs[:, QC * lo:QC * hi],
-                             T.xb[:, XC * lo:XC * hi]).then_inc(T.sem["qd%d" % k], 1)
-    g.vector.wait_ge(T.sem["ld%d" % own], 16)
-    for d in peers:
-        g.vector.quantize_mx(T.xq[:, QC * d:QC * (d + 1)], T.xs[:, QC * d:QC * (d + 1)],
-                             T.xb[:, XC * d:XC * (d + 1)]).then_inc(T.sem["qd%d" % own], 1)
-    g.vector.quantize_mx(T.rq[:, QC * r:QC * (r + 1)], T.rs[:, QC * r:QC * (r + 1)],
-                         T.xb[:, XC * r:XC * (r + 1)]).then_inc(T.sem.qme, 1)
+    for i, (lo, hi) in enumerate(pieces):
+        g.vector.wait_ge(T.sem["ld%d" % i], 16)
+        if i < len(pieces) - 1:
+            g.vector.quantize_mx(T.xq[:, QC * lo:QC * hi], T.xs[:, QC * lo:QC * hi],
+                                 T.xb[:, XC * lo:XC * hi]).then_inc(T.sem["qd%d" % i], 1)
+            continue
+        for d in range(lo, hi):
+            if d != r:
+                g.vector.quantize_mx(T.xq[:, QC * d:QC * (d + 1)], T.xs[:, QC * d:QC * (d + 1)],
+                                     T.xb[:, XC * d:XC * (d + 1)]).then_inc(T.sem["qd%d" % i], 1)
+        g.vector.quantize_mx(T.rq[:, QC * r:QC * (r + 1)], T.rs[:, QC * r:QC * (r + 1)],
+                             T.xb[:, XC * r:XC * (r + 1)]).then_inc(T.sem.qme, 1)
     g.vector.wait_ge(T.sem.ldw, 16)
     g.vector.quantize_mx(T.wq[:], T.ws[:], T.wb[:]).then_inc(T.sem.qw, 1)
 
-    left = 0
-    for k in far:
-        g.wait_ge(T.sem["qd%d" % k], 1)
-    masks = _split(topo, core, [relay[(r, k)] for k in far])
-    for view, buf, sem in ((_plane, T.xs, T.sem.hs), (_codes, T.xq, T.sem.hq)):
-        g.remote_dma_fused([_xfer(topo, core, relay[(r, k)], masks[relay[(r, k)]], sem,
-                                  view(buf, span[k][0], span[k][1]), view(buf, span[k][0], span[k][1]))
-                            for k in far], local_sem=T.sem.sent)
-        left += sum(_count(masks[relay[(r, k)]]) for k in far)
-    for k in near:
-        g.wait_ge(T.sem["qd%d" % k], 1)
-    g.wait_ge(T.sem["qd%d" % own], len(peers))
-    dsts = _own_dsts(cores, groups, relay, r)
-    masks = _split(topo, core, [cores[d] for d in dsts])
-    for view, here, there in ((_codes, T.xq, T.rq), (_plane, T.xs, T.rs)):
-        g.remote_dma_fused([_xfer(topo, core, cores[d], masks[cores[d]], T.sem["arr%d" % own],
-                                  view(here, d, d + 1), view(there, r, r + 1))
-                            for d in dsts], local_sem=T.sem.sent)
-        left += sum(_count(masks[cores[d]]) for d in dsts)
+    left = _issue(g, core, T, topo, calls, landed)
 
     g.tensor.wait_ge(T.sem.qw, 1)
     for i, k in enumerate([own] + near + far):
-        lo, hi = span[k]
-        due = sum(2 * _count(_last_hop(cores, topo, groups, relay, j, own)[core]) for j in groups[k] if j != r)
-        g.tensor.wait_ge(T.sem["arr%d" % k], due)
+        g.tensor.wait_ge(T.sem["arr%d" % k], landed[(core, "arr%d" % k)])
         if k == own:
             g.tensor.wait_ge(T.sem.qme, 1)
-        bank = T.ps[:, BANK * k:BANK * k + QC * (hi - lo)]
-        g.tensor.matmul_mx(bank, T.wq[:], T.ws[:], T.rq[:, QC * lo:QC * hi], T.rs[:, QC * lo:QC * hi],
-                           True, True).then_inc(T.sem["mm%d" % k], 1)
-        out = T.yb[:, QC * lo:QC * hi]
-        if i % 2 == 0:
-            g.vector.wait_ge(T.sem["mm%d" % k], 1)
-            g.vector.tensor_copy(out, bank).then_inc(T.sem["cp%d" % k], 1)
-        else:
-            g.scalar.wait_ge(T.sem["mm%d" % k], 1)
-            g.scalar.activation(out, bank, ActivationFunctionType.Copy).then_inc(T.sem["cp%d" % k], 1)
-        hw[i % 2].wait_ge(T.sem["cp%d" % k], 1)
-        hw[i % 2].dma_start(T.y[:, QC * lo:QC * hi], out).then_inc(T.sem.st, 16)
+        for n, j in enumerate(groups[k]):
+            bank = T.ps[:, BANK * j:BANK * j + QC]
+            g.tensor.matmul_mx(bank, T.wq[:], T.ws[:], T.rq[:, QC * j:QC * (j + 1)], T.rs[:, QC * j:QC * (j + 1)],
+                               True, True).then_inc(T.sem["mm%d" % j], 1)
+            out = T.yb[:, QC * j:QC * (j + 1)]
+            if n % 2 == 0:
+                g.vector.wait_ge(T.sem["mm%d" % j], 1)
+                g.vector.tensor_copy(out, bank).then_inc(T.sem["cp%d" % j], 1)
+            else:
+                g.scalar.wait_ge(T.sem["mm%d" % j], 1)
+                g.scalar.activation(out, bank, ActivationFunctionType.Copy).then_inc(T.sem["cp%d" % j], 1)
+        for j in groups[k]:
+            hw[i % 2].wait_ge(T.sem["cp%d" % j], 1)
+        lo, hi = groups[k][0], groups[k][-1] + 1
+        hw[i % 2].dma_start(T.y[:, QC * lo:QC * hi], T.yb[:, QC * lo:QC * hi]).then_inc(T.sem.st, 16)
 
     g.wait_ge(T.sem.sent, left)
     g.wait_ge(T.sem.st, 16 * len(groups))

from concourse.bass import DstId, RemoteDMATransfer
from concourse.mybir import dt, ActivationFunctionType

N = 8
NG = 4
NP = 6
WORLD = 256
XC = 512
QC = 128
BANK = 512

SCRATCH = {
    "xb": ("sbuf", [128, N * XC], "bfloat16"),
    "wb": ("sbuf", [128, XC], "bfloat16"),
    "xq": ("sbuf", [128, N * QC], "float8_e4m3fn_x4"),
    "xs": ("sbuf", [128, N * QC], "uint8"),
    "wq": ("sbuf", [128, QC], "float8_e4m3fn_x4"),
    "ws": ("sbuf", [128, QC], "uint8"),
    "rq": ("sbuf", [128, N * QC], "float8_e4m3fn_x4"),
    "rs": ("sbuf", [128, N * QC], "uint8"),
    "ps": ("psum", [128, N * BANK], "float32"),
    "yb": ("sbuf", [128, N * QC], "float32"),
}
SEMAPHORES = (["ld%d" % i for i in range(NP)] + ["qd%d" % i for i in range(NP)] + ["arr%d" % k for k in range(NG)]
              + ["mm%d" % j for j in range(N)] + ["cp%d" % j for j in range(N)]
              + ["ldw", "qw", "qme", "hlead", "hrest", "hcodes", "sent", "st"])


def _count(mask):
    return bin(mask).count("1")


def _plan(cores, topo):
    groups = []
    for r, c in enumerate(cores):
        for gr in groups:
            if topo.host(cores[gr[0]]) == topo.host(c) and topo.chip(cores[gr[0]]) == topo.chip(c):
                gr.append(r)
                break
        else:
            groups.append([r])
    relay, taken = {}, set(cores)
    for j, c in enumerate(cores):
        for k, gr in enumerate(groups):
            if all(topo.may_write(c, cores[d]) for d in gr):
                continue
            idle = [h for h in range(WORLD) if h not in taken
                    and topo.host(h) == topo.host(c) and topo.chip(h) == topo.chip(c)
                    and all(topo.may_write(h, cores[d]) for d in gr)]
            idle.sort(key=lambda h: topo.die(h) != topo.die(c))
            relay[(j, k)] = idle[0]
            taken.add(idle[0])
    return groups, relay


def _split(topo, src, dsts):
    masks, taken = {}, 0
    for m in sorted(set(topo.mask(src, d) for d in dsts), key=_count):
        those = [d for d in dsts if topo.mask(src, d) == m]
        free = [b for b in range(m.bit_length()) if ((m & ~taken) >> b) & 1]
        n = 1
        while 2 * n * len(those) <= len(free):
            n *= 2
        for i, d in enumerate(those):
            masks[d] = sum(1 << b for b in free[i * n:(i + 1) * n])
            taken |= masks[d]
    return masks


def _roles(cores, topo, groups, relay, j):
    own = [k for k, gr in enumerate(groups) if j in gr][0]
    far = [k for k in range(len(groups)) if (j, k) in relay]
    far.sort(key=lambda k: topo.host(cores[groups[k][0]]) != topo.host(cores[j]))
    near = [k for k in range(len(groups)) if k != own and k not in far]
    pieces = ([(groups[k][0], groups[k][0] + 1) for k in far] + [(groups[k][1], groups[k][-1] + 1) for k in far]
              + [(groups[k][0], groups[k][-1] + 1) for k in near + [own]])
    return own, far, near, pieces


def _remote_calls(cores, topo, groups, relay):
    calls = {}
    for j, c in enumerate(cores):
        own, far, near, pieces = _roles(cores, topo, groups, relay, j)
        nf = len(far)
        mine = []
        for i, k in enumerate(far):
            lo, hi = pieces[i]
            h = relay[(j, k)]
            mine.append(([("qd%d" % i, 1)], [(h, topo.mask(c, h), "hlead", "s", lo, hi, "x", lo)]))
        m = _split(topo, c, [relay[(j, k)] for k in far])
        mine.append(([("qd%d" % (nf + i), 1) for i in range(nf)],
                     [(relay[(j, k)], m[relay[(j, k)]], "hrest", "s", pieces[nf + i][0], pieces[nf + i][1], "x", pieces[nf + i][0])
                      for i, k in enumerate(far)]))
        mine.append(([], [(relay[(j, k)], m[relay[(j, k)]], "hcodes", "q", groups[k][0], groups[k][-1] + 1, "x", groups[k][0])
                          for k in far]))
        dsts = [d for k in near + [own] for d in groups[k] if d != j]
        m = _split(topo, c, [cores[d] for d in dsts])
        waits = [("qd%d" % (2 * nf + i), 1) for i in range(len(near))] + [("qd%d" % (2 * nf + len(near)), len(groups[own]) - 1)]
        for kind in "qs":
            mine.append((waits, [(cores[d], m[cores[d]], "arr%d" % own, kind, d, d + 1, "r", j) for d in dsts]))
            waits = []
        calls[c] = mine
        for k in far:
            h, gr = relay[(j, k)], groups[k]
            arr = "arr%d" % own
            rest = _split(topo, h, [cores[d] for d in gr[1:]])
            both = _split(topo, h, [cores[d] for d in gr])
            calls[h] = [([("hlead", None)], [(cores[gr[0]], topo.mask(h, cores[gr[0]]), arr, "s", gr[0], gr[0] + 1, "r", j)]),
                        ([("hrest", None)], [(cores[d], rest[cores[d]], arr, "s", d, d + 1, "r", j) for d in gr[1:]]),
                        ([("hcodes", None)], [(cores[d], both[cores[d]], arr, "q", d, d + 1, "r", j) for d in gr])]
    landed = {}
    for c in calls:
        for waits, transfers in calls[c]:
            for t in transfers:
                landed[(t[0], t[2])] = landed.get((t[0], t[2]), 0) + _count(t[1])
    return calls, landed


def _view(buf, kind, lo, hi):
    return buf[:, QC * lo:QC * hi].bitcast(dt.uint8) if kind == "q" else buf[:, QC * lo:QC * hi]


def _issue(g, core, T, topo, calls, landed):
    left = 0
    for waits, transfers in calls[core]:
        for name, count in waits:
            g.wait_ge(T.sem[name], landed[(core, name)] if count is None else count)
        made = []
        for dst, mask, sem, kind, lo, hi, there, at in transfers:
            rid, pid = topo.addr(dst, core)
            made.append(RemoteDMATransfer(dst_ids=[DstId(rid=rid, pnc=pid)], dma_engine_mask=mask, remote_sem=T.sem[sem],
                                          src=_view(T["x" + kind], kind, lo, hi),
                                          dst=_view(T[there + kind], kind, at, at + hi - lo)))
            left += _count(mask)
        g.remote_dma_fused(made, local_sem=T.sem.sent)
    return left


def rank_program(g, core, T, topo):
    cores = [int(c) for c in T.cores]
    groups, relay = _plan(cores, topo)
    calls, landed = _remote_calls(cores, topo, groups, relay)
    if core not in calls:
        return
    r = T.rank_of(core)
    if r is None:
        g.wait_ge(T.sem.sent, _issue(g, core, T, topo, calls, landed))
        return

    own, far, near, pieces = _roles(cores, topo, groups, relay, r)
    hw = (g.sync, g.scalar)

    for i, (lo, hi) in enumerate(pieces):
        hw[i % 2].dma_start(T.xb[:, XC * lo:XC * hi], T.x[:, XC * lo:XC * hi]).then_inc(T.sem["ld%d" % i], 16)
    hw[len(pieces) % 2].dma_start(T.wb[:], T.w[:]).then_inc(T.sem.ldw, 16)

    for i, (lo, hi) in enumerate(pieces):
        g.vector.wait_ge(T.sem["ld%d" % i], 16)
        if i < len(pieces) - 1:
            g.vector.quantize_mx(T.xq[:, QC * lo:QC * hi], T.xs[:, QC * lo:QC * hi],
                                 T.xb[:, XC * lo:XC * hi]).then_inc(T.sem["qd%d" % i], 1)
            continue
        for d in range(lo, hi):
            if d != r:
                g.vector.quantize_mx(T.xq[:, QC * d:QC * (d + 1)], T.xs[:, QC * d:QC * (d + 1)],
                                     T.xb[:, XC * d:XC * (d + 1)]).then_inc(T.sem["qd%d" % i], 1)
        g.vector.quantize_mx(T.rq[:, QC * r:QC * (r + 1)], T.rs[:, QC * r:QC * (r + 1)],
                             T.xb[:, XC * r:XC * (r + 1)]).then_inc(T.sem.qme, 1)
    g.vector.wait_ge(T.sem.ldw, 16)
    g.vector.quantize_mx(T.wq[:], T.ws[:], T.wb[:]).then_inc(T.sem.qw, 1)

    left = _issue(g, core, T, topo, calls, landed)

    g.tensor.wait_ge(T.sem.qw, 1)
    for i, k in enumerate([own] + near + far):
        g.tensor.wait_ge(T.sem["arr%d" % k], landed[(core, "arr%d" % k)])
        if k == own:
            g.tensor.wait_ge(T.sem.qme, 1)
        for n, j in enumerate(groups[k]):
            bank = T.ps[:, BANK * j:BANK * j + QC]
            g.tensor.matmul_mx(bank, T.wq[:], T.ws[:], T.rq[:, QC * j:QC * (j + 1)], T.rs[:, QC * j:QC * (j + 1)],
                               True, True).then_inc(T.sem["mm%d" % j], 1)
            out = T.yb[:, QC * j:QC * (j + 1)]
            if n % 2 == 0:
                g.vector.wait_ge(T.sem["mm%d" % j], 1)
                g.vector.tensor_copy(out, bank).then_inc(T.sem["cp%d" % j], 1)
            else:
                g.scalar.wait_ge(T.sem["mm%d" % j], 1)
                g.scalar.activation(out, bank, ActivationFunctionType.Copy).then_inc(T.sem["cp%d" % j], 1)
        for j in groups[k]:
            hw[i % 2].wait_ge(T.sem["cp%d" % j], 1)
        lo, hi = groups[k][0], groups[k][-1] + 1
        hw[i % 2].dma_start(T.y[:, QC * lo:QC * hi], T.yb[:, QC * lo:QC * hi]).then_inc(T.sem.st, 16)

    g.wait_ge(T.sem.sent, left)
    g.wait_ge(T.sem.st, 16 * len(groups))
